import numpy as np, ml_dtypes
CORES = [4,12,20,132,140,148,260,268,276,388,396,404]
N = 12
F = 128
def setup_inputs(rng):
    return {"a": rng.standard_normal((N, 128, N * 128), dtype=np.float32).astype(ml_dtypes.bfloat16), "w": rng.standard_normal((N, 128, F), dtype=np.float32).astype(ml_dtypes.bfloat16)}
def reference(a, w):
    tot = np.zeros((N * 128, F))
    for j in range(N):
        tot += a[j].astype(np.float64).T @ w[j].astype(np.float64)
    return {"y": np.stack([tot[128 * r:128 * r + 128] for r in range(N)]).astype(ml_dtypes.bfloat16 if a.dtype != np.float64 else np.float64)}

@@ -1,0 +1,213 @@
+from concourse.bass import DstId, RemoteDMATransfer
+from concourse.mybir import dt, AluOpType
+
+NSIM = 512
+B = 128
+
+SCRATCH = {
+    "a_sb": ("sbuf", [128, 12 * B], "bfloat16"),
+    "w_sb": ("sbuf", [128, B], "bfloat16"),
+    "bund": ("sbuf", [128, 12 * B], "bfloat16"),
+    "land": ("sbuf", [128, 12 * B], "bfloat16"),
+    "fin": ("sbuf", [128, 4 * B], "bfloat16"),
+    "y_sb": ("sbuf", [128, B], "bfloat16"),
+    "ps0": ("psum", [128, 512], "float32"),
+    "ps1": ("psum", [128, 512], "float32"),
+    "ps2": ("psum", [128, 512], "float32"),
+    "ps3": ("psum", [128, 512], "float32"),
+    "ps4": ("psum", [128, 512], "float32"),
+}
+SEMAPHORES = ["ldw", "ldf", "ldn", "mm0", "mm1", "mm2", "mm3", "cpf", "cpn", "sent", "vs", "st",
+              "got0", "got1", "got2", "got3", "arr0", "arr1", "arr2", "arr3"]
+
+_CACHE = {}
+
+
+def _pop(m):
+    return bin(m).count("1")
+
+
+def _bits(m):
+    return [1 << i for i in range(m.bit_length()) if (m >> i) & 1]
+
+
+def _split(bits, n):
+    L = len(bits)
+    sizes = {1: [L], 2: [L // 2] * 2, 3: [L // 2, L // 4, L // 4], 4: [L // 4] * 4}[n]
+    out, p = [], 0
+    for s in sizes:
+        out.append(sum(bits[p:p + s]))
+        p += s
+    return out
+
+
+def _masks(topo, src, dsts):
+    full = [topo.mask(src, d) for d in dsts]
+    tight = min(full, key=_pop)
+    res = [0] * len(dsts)
+    out = [i for i, m in enumerate(full) if m == tight]
+    loc = [i for i, m in enumerate(full) if m != tight]
+    for i, m in zip(out, _split(_bits(tight), len(out))):
+        res[i] = m
+    if loc:
+        for i, m in zip(loc, _split(_bits(full[loc[0]] & ~tight), len(loc))):
+            res[i] = m
+    return res
+
+
+def _plan(T, topo):
+    if "p" in _CACHE:
+        return _CACHE["p"]
+    cores = list(T.cores)
+    hosts = sorted({topo.host(c) for c in cores})
+    members = {H: [c for c in cores if topo.host(c) == H] for H in hosts}
+
+    def rack(c):
+        return topo.rack(topo.host(c))
+
+    def same_chip(x, y):
+        return topo.host(x) == topo.host(y) and topo.chip(x) == topo.chip(y)
+
+    def hops(c, d):
+        if same_chip(c, d):
+            return 0
+        if rack(c) == rack(d):
+            return 1 if (topo.mates(c, d) or topo.same_plane(c, d)) else 2
+        twin = [x for x in range(NSIM) if topo.host(x) == topo.host(d) and topo.chip(x) == topo.chip(c)][0]
+        return 1 + hops(twin, d)
+
+    classes = []
+    for R in sorted({rack(c) for c in cores}):
+        left = [c for c in cores if rack(c) == R]
+        while left:
+            k = [c for c in left if c == left[0] or topo.may_write(left[0], c)]
+            classes.append(k)
+            left = [c for c in left if c not in k]
+
+    used, load, agg = set(cores), {}, {}
+    for far in (True, False):
+        for ci, k in enumerate(classes):
+            for H in hosts:
+                if (topo.rack(H) != rack(k[0])) != far:
+                    continue
+                cand = [x for x in range(NSIM) if x not in used and any(same_chip(x, s) for s in k)
+                        and all(topo.may_write(x, d) for d in members[H]) and all(topo.may_write(s, x) for s in k)]
+                best = min(cand, key=lambda x: (load.get((topo.host(x), topo.chip(x)), 0),
+                                                sum(hops(x, d) for d in members[H]),
+                                                topo.die(x) != topo.die(k[0]), x))
+                used.add(best)
+                load[(topo.host(best), topo.chip(best))] = load.get((topo.host(best), topo.chip(best)), 0) + 1
+                agg[(ci, H)] = best
+
+    hop1 = {}
+    for ci, k in enumerate(classes):
+        for slot, s in enumerate(k):
+            calls = []
+            for far in (True, False):
+                hs = [H for H in hosts if (topo.rack(H) != rack(s)) == far]
+                ms = _masks(topo, s, [agg[(ci, H)] for H in hs])
+                calls.append([(H, agg[(ci, H)], slot, m) for H, m in zip(hs, ms)])
+            hop1[s] = calls
+    hop2 = {}
+    for (ci, H), x in agg.items():
+        order = sorted(range(len(members[H])), key=lambda j: (-hops(x, members[H][j]), j))
+        ms = _masks(topo, x, [members[H][j] for j in order])
+        hop2[x] = (ci, H, [(j, members[H][j], m) for j, m in zip(order, ms)])
+    p = dict(hosts=hosts, members=members, classes=classes, agg=agg, hop1=hop1, hop2=hop2, same_chip=same_chip, rack=rack)
+    _CACHE["p"] = p
+    return p
+
+
+def _dst(topo, d, src):
+    rid, pid = topo.addr(d, src)
+    return DstId(rid=rid, pnc=pid)
+
+
+def _aggregator(g, core, T, topo, p):
+    ci, H, sends = p["hop2"][core]
+    k = p["classes"][ci]
+    W = B * len(p["members"][H])
+    cnt = [[_pop(m) for call in p["hop1"][s] for (h, x, sl, m) in call if x == core][0] for s in k]
+    order = sorted(range(len(k)), key=lambda i: (not p["same_chip"](k[i], core), i))
+    v = g.vector
+    ps = [T.ps0, T.ps1]
+    i = order[0]
+    v.wait_ge(T.sem["got%d" % i], cnt[i])
+    v.tensor_copy(ps[0][:, 0:W], T.land[:, i * W:(i + 1) * W]).then_inc(T.sem.vs, 1)
+    for t, i in enumerate(order[1:], 1):
+        v.wait_ge(T.sem["got%d" % i], cnt[i])
+        v.wait_ge(T.sem.vs, t)
+        out = T.bund[:, 0:W] if t == len(k) - 1 else ps[t % 2][:, 0:W]
+        v.tensor_tensor(out, ps[(t - 1) % 2][:, 0:W], T.land[:, i * W:(i + 1) * W], AluOpType.add).then_inc(T.sem.vs, 1)
+    g.wait_ge(T.sem.vs, len(k))
+    g.remote_dma_fused([RemoteDMATransfer(dst_ids=[_dst(topo, d, core)], dma_engine_mask=m, remote_sem=T.sem["arr%d" % ci],
+                                          src=T.bund[:, j * B:(j + 1) * B], dst=T.fin[:, ci * B:(ci + 1) * B])
+                        for (j, d, m) in sends], local_sem=T.sem.sent)
+    g.wait_ge(T.sem.sent, sum(_pop(m) for (j, d, m) in sends))
+
+
+def _rank(g, core, T, topo, p):
+    members, classes = p["members"], p["classes"]
+    calls = p["hop1"][core]
+
+    def cols(H):
+        r0 = T.rank_of(members[H][0])
+        return r0 * B, (r0 + len(members[H])) * B
+
+    span = []
+    for call in calls:
+        lo = min(cols(H)[0] for (H, x, sl, m) in call)
+        hi = max(cols(H)[1] for (H, x, sl, m) in call)
+        span.append((lo, hi))
+    g.scalar.dma_start(T.w_sb[:], T.w[:]).then_inc(T.sem.ldw, 16)
+    g.sync.dma_start(T.a_sb[:, span[0][0]:span[0][1]], T.a[:, span[0][0]:span[0][1]]).then_inc(T.sem.ldf, 16)
+    g.scalar.dma_start(T.a_sb[:, span[1][0]:span[1][1]], T.a[:, span[1][0]:span[1][1]]).then_inc(T.sem.ldn, 16)
+    g.tensor.wait_ge(T.sem.ldw, 16)
+    n = 0
+    for c, call in enumerate(calls):
+        g.tensor.wait_ge(T.sem.ldf if c == 0 else T.sem.ldn, 16)
+        for (H, x, sl, m) in call:
+            lo, hi = cols(H)
+            ps = T["ps%d" % n]
+            for q in range(lo, hi, B):
+                g.tensor.matmul(ps[:, q - lo:q - lo + B], T.a_sb[:, q:q + B], T.w_sb[:], True, True).then_inc(T.sem["mm%d" % n], 1)
+            g.vector.wait_ge(T.sem["mm%d" % n], (hi - lo) // B)
+            g.vector.tensor_copy(T.bund[:, lo:hi], ps[:, 0:hi - lo]).then_inc(T.sem.cpf if c == 0 else T.sem.cpn, 1)
+            n += 1
+    total = 0
+    for c, call in enumerate(calls):
+        g.wait_ge(T.sem.cpf if c == 0 else T.sem.cpn, len(call))
+        trs = []
+        for (H, x, sl, m) in call:
+            lo, hi = cols(H)
+            trs.append(RemoteDMATransfer(dst_ids=[_dst(topo, x, core)], dma_engine_mask=m, remote_sem=T.sem["got%d" % sl],
+                                         src=T.bund[:, lo:hi], dst=T.land[:, sl * (hi - lo):(sl + 1) * (hi - lo)]))
+            total += _pop(m)
+        g.remote_dma_fused(trs, local_sem=T.sem.sent)
+    H = topo.host(core)
+    cnt = {}
+    for ci in range(len(classes)):
+        cnt[ci] = [_pop(m) for (j, d, m) in p["hop2"][p["agg"][(ci, H)]][2] if d == core][0]
+    order = sorted(range(len(classes)), key=lambda ci: (p["rack"](classes[ci][0]) != p["rack"](core), len(classes[ci]), ci))
+    v = g.vector
+    f = [T.fin[:, ci * B:(ci + 1) * B] for ci in order]
+    v.wait_ge(T.sem["arr%d" % order[0]], cnt[order[0]])
+    v.wait_ge(T.sem["arr%d" % order[1]], cnt[order[1]])
+    v.tensor_tensor(T.ps4[:, 0:B], f[0], f[1], AluOpType.add).then_inc(T.sem.vs, 1)
+    for t in range(2, len(order)):
+        v.wait_ge(T.sem["arr%d" % order[t]], cnt[order[t]])
+        v.wait_ge(T.sem.vs, t - 1)
+        out = T.y_sb[:] if t == len(order) - 1 else T.ps4[:, (t - 1) * B:t * B]
+        v.tensor_tensor(out, T.ps4[:, (t - 2) * B:(t - 1) * B], f[t], AluOpType.add).then_inc(T.sem.vs, 1)
+    g.sync.wait_ge(T.sem.vs, len(order) - 1)
+    g.sync.dma_start(T.y[:], T.y_sb[:]).then_inc(T.sem.st, 16)
+    g.sync.wait_ge(T.sem.st, 16)
+    g.wait_ge(T.sem.sent, total)
+
+
+def rank_program(g, core, T, topo):
+    p = _plan(T, topo)
+    if T.rank_of(core) is not None:
+        _rank(g, core, T, topo, p)
+    elif core in p["hop2"]:
+        _aggregator(g, core, T, topo, p)

@@ -8,8 +8,8 @@ SCRATCH = {
     "a_sb": ("sbuf", [128, 12 * B], "bfloat16"),
     "w_sb": ("sbuf", [128, B], "bfloat16"),
     "bund": ("sbuf", [128, 12 * B], "bfloat16"),
-    "land": ("sbuf", [128, 12 * B], "bfloat16"),
-    "fin": ("sbuf", [128, 4 * B], "bfloat16"),
+    "land": ("sbuf", [128, 6 * B], "bfloat16"),
+    "fin": ("sbuf", [128, 6 * B], "bfloat16"),
     "y_sb": ("sbuf", [128, B], "bfloat16"),
     "ps0": ("psum", [128, 512], "float32"),
     "ps1": ("psum", [128, 512], "float32"),
@@ -18,7 +18,7 @@ SCRATCH = {
     "ps4": ("psum", [128, 512], "float32"),
 }
 SEMAPHORES = ["ldw", "ldf", "ldn", "mm0", "mm1", "mm2", "mm3", "cpf", "cpn", "sent", "vs", "st",
-              "got0", "got1", "got2", "got3", "arr0", "arr1", "arr2", "arr3"]
+              "got0", "got1", "arr0", "arr1", "arr2", "arr3", "arr4", "arr5"]
 
 _CACHE = {}
 
@@ -76,17 +76,17 @@ def _plan(T, topo):
         twin = [x for x in range(NSIM) if topo.host(x) == topo.host(d) and topo.chip(x) == topo.chip(c)][0]
         return 1 + hops(twin, d)
 
-    classes = []
+    pairs = []
     for R in sorted({rack(c) for c in cores}):
         left = [c for c in cores if rack(c) == R]
         while left:
-            k = [c for c in left if c == left[0] or topo.may_write(left[0], c)]
-            classes.append(k)
+            k = [c for c in left if c == left[0] or (topo.chip(c) == topo.chip(left[0]) and topo.may_write(left[0], c))]
+            pairs.append(k)
             left = [c for c in left if c not in k]
 
     used, load, agg = set(cores), {}, {}
     for far in (True, False):
-        for ci, k in enumerate(classes):
+        for ci, k in enumerate(pairs):
             for H in hosts:
                 if (topo.rack(H) != rack(k[0])) != far:
                     continue
@@ -100,7 +100,7 @@ def _plan(T, topo):
                 agg[(ci, H)] = best
 
     hop1 = {}
-    for ci, k in enumerate(classes):
+    for ci, k in enumerate(pairs):
         for slot, s in enumerate(k):
             calls = []
             for far in (True, False):
@@ -113,7 +113,7 @@ def _plan(T, topo):
         order = sorted(range(len(members[H])), key=lambda j: (-hops(x, members[H][j]), j))
         ms = _masks(topo, x, [members[H][j] for j in order])
         hop2[x] = (ci, H, [(j, members[H][j], m) for j, m in zip(order, ms)])
-    p = dict(hosts=hosts, members=members, classes=classes, agg=agg, hop1=hop1, hop2=hop2, same_chip=same_chip, rack=rack)
+    p = dict(hosts=hosts, members=members, pairs=pairs, agg=agg, hop1=hop1, hop2=hop2, same_chip=same_chip, rack=rack, hops=hops)
     _CACHE["p"] = p
     return p
 
@@ -125,10 +125,11 @@ def _dst(topo, d, src):
 
 def _aggregator(g, core, T, topo, p):
     ci, H, sends = p["hop2"][core]
-    k = p["classes"][ci]
+    k = p["pairs"][ci]
+    n = len(k)
     W = B * len(p["members"][H])
     cnt = [[_pop(m) for call in p["hop1"][s] for (h, x, sl, m) in call if x == core][0] for s in k]
-    order = sorted(range(len(k)), key=lambda i: (not p["same_chip"](k[i], core), i))
+    order = sorted(range(n), key=lambda i: (not p["same_chip"](k[i], core), i))
     v = g.vector
     ps = [T.ps0, T.ps1]
     i = order[0]
@@ -137,9 +138,9 @@ def _aggregator(g, core, T, topo, p):
     for t, i in enumerate(order[1:], 1):
         v.wait_ge(T.sem["got%d" % i], cnt[i])
         v.wait_ge(T.sem.vs, t)
-        out = T.bund[:, 0:W] if t == len(k) - 1 else ps[t % 2][:, 0:W]
+        out = T.bund[:, 0:W] if t == n - 1 else ps[t % 2][:, 0:W]
         v.tensor_tensor(out, ps[(t - 1) % 2][:, 0:W], T.land[:, i * W:(i + 1) * W], AluOpType.add).then_inc(T.sem.vs, 1)
-    g.wait_ge(T.sem.vs, len(k))
+    g.wait_ge(T.sem.vs, n)
     g.remote_dma_fused([RemoteDMATransfer(dst_ids=[_dst(topo, d, core)], dma_engine_mask=m, remote_sem=T.sem["arr%d" % ci],
                                           src=T.bund[:, j * B:(j + 1) * B], dst=T.fin[:, ci * B:(ci + 1) * B])
                         for (j, d, m) in sends], local_sem=T.sem.sent)
@@ -147,7 +148,7 @@ def _aggregator(g, core, T, topo, p):
 
 
 def _rank(g, core, T, topo, p):
-    members, classes = p["members"], p["classes"]
+    members, pairs = p["members"], p["pairs"]
     calls = p["hop1"][core]
 
     def cols(H):
@@ -186,9 +187,10 @@ def _rank(g, core, T, topo, p):
         g.remote_dma_fused(trs, local_sem=T.sem.sent)
     H = topo.host(core)
     cnt = {}
-    for ci in range(len(classes)):
+    for ci in range(len(pairs)):
         cnt[ci] = [_pop(m) for (j, d, m) in p["hop2"][p["agg"][(ci, H)]][2] if d == core][0]
-    order = sorted(range(len(classes)), key=lambda ci: (p["rack"](classes[ci][0]) != p["rack"](core), len(classes[ci]), ci))
+    order = sorted(range(len(pairs)), key=lambda ci: (p["rack"](pairs[ci][0]) != p["rack"](core),
+                                                      p["hops"](p["agg"][(ci, H)], core), -cnt[ci], ci))
     v = g.vector
     f = [T.fin[:, ci * B:(ci + 1) * B] for ci in order]
     v.wait_ge(T.sem["arr%d" % order[0]], cnt[order[0]])

@@ -3,21 +3,21 @@ from concourse.mybir import dt, AluOpType
 
 NSIM = 512
 B = 128
+G = 3 * B
+P = G + B
 
 SCRATCH = {
-    "a_sb": ("sbuf", [128, 12 * B], "bfloat16"),
-    "w_sb": ("sbuf", [128, B], "bfloat16"),
-    "bund": ("sbuf", [128, 12 * B], "bfloat16"),
-    "land": ("sbuf", [128, 6 * B], "bfloat16"),
+    "ab": ("sbuf", [128, 2 * (G + P)], "bfloat16"),
+    "land": ("sbuf", [128, 2 * P], "bfloat16"),
+    "bund": ("sbuf", [128, G], "bfloat16"),
     "fin": ("sbuf", [128, 6 * B], "bfloat16"),
     "y_sb": ("sbuf", [128, B], "bfloat16"),
     "ps0": ("psum", [128, 512], "float32"),
     "ps1": ("psum", [128, 512], "float32"),
     "ps2": ("psum", [128, 512], "float32"),
-    "ps3": ("psum", [128, 512], "float32"),
     "ps4": ("psum", [128, 512], "float32"),
 }
-SEMAPHORES = ["ldw", "ldf", "ldn", "mm0", "mm1", "mm2", "mm3", "cpf", "cpn", "sent", "vs", "st",
+SEMAPHORES = ["ldf", "ldn", "mm0", "mm1", "mm2", "sent", "vs", "st",
               "got0", "got1", "arr0", "arr1", "arr2", "arr3", "arr4", "arr5"]
 
 _CACHE = {}
@@ -127,20 +127,23 @@ def _aggregator(g, core, T, topo, p):
     ci, H, sends = p["hop2"][core]
     k = p["pairs"][ci]
     n = len(k)
-    W = B * len(p["members"][H])
     cnt = [[_pop(m) for call in p["hop1"][s] for (h, x, sl, m) in call if x == core][0] for s in k]
+    pos = [[q for call in p["hop1"][s] for q, (h, x, sl, m) in enumerate(call) if x == core][0] for s in k]
     order = sorted(range(n), key=lambda i: (not p["same_chip"](k[i], core), i))
-    v = g.vector
-    ps = [T.ps0, T.ps1]
-    i = order[0]
-    v.wait_ge(T.sem["got%d" % i], cnt[i])
-    v.tensor_copy(ps[0][:, 0:W], T.land[:, i * W:(i + 1) * W]).then_inc(T.sem.vs, 1)
-    for t, i in enumerate(order[1:], 1):
-        v.wait_ge(T.sem["got%d" % i], cnt[i])
-        v.wait_ge(T.sem.vs, t)
-        out = T.bund[:, 0:W] if t == n - 1 else ps[t % 2][:, 0:W]
-        v.tensor_tensor(out, ps[(t - 1) % 2][:, 0:W], T.land[:, i * W:(i + 1) * W], AluOpType.add).then_inc(T.sem.vs, 1)
-    g.wait_ge(T.sem.vs, n)
+    js = [j for (j, d, m) in sends]
+    for t, i in enumerate(order):
+        g.tensor.wait_ge(T.sem["got%d" % i], cnt[i])
+        a0 = i * P + (0 if pos[i] == 0 else B)
+        w0 = i * P + (G if pos[i] == 0 else 0)
+        for j in js:
+            mm = g.tensor.matmul(T["ps%d" % j][:, 0:B], T.land[:, a0 + j * B:a0 + (j + 1) * B], T.land[:, w0:w0 + B],
+                                 t == 0, t == n - 1)
+            if t == n - 1:
+                mm.then_inc(T.sem["mm%d" % j], 1)
+    for j in js:
+        g.vector.wait_ge(T.sem["mm%d" % j], 1)
+        g.vector.tensor_copy(T.bund[:, j * B:(j + 1) * B], T["ps%d" % j][:, 0:B]).then_inc(T.sem.vs, 1)
+    g.wait_ge(T.sem.vs, len(js))
     g.remote_dma_fused([RemoteDMATransfer(dst_ids=[_dst(topo, d, core)], dma_engine_mask=m, remote_sem=T.sem["arr%d" % ci],
                                           src=T.bund[:, j * B:(j + 1) * B], dst=T.fin[:, ci * B:(ci + 1) * B])
                         for (j, d, m) in sends], local_sem=T.sem.sent)
@@ -153,36 +156,25 @@ def _rank(g, core, T, topo, p):
 
     def cols(H):
         r0 = T.rank_of(members[H][0])
-        return r0 * B, (r0 + len(members[H])) * B
+        return r0 * B, r0 * B + G
 
-    span = []
-    for call in calls:
-        lo = min(cols(H)[0] for (H, x, sl, m) in call)
-        hi = max(cols(H)[1] for (H, x, sl, m) in call)
-        span.append((lo, hi))
-    g.scalar.dma_start(T.w_sb[:], T.w[:]).then_inc(T.sem.ldw, 16)
-    g.sync.dma_start(T.a_sb[:, span[0][0]:span[0][1]], T.a[:, span[0][0]:span[0][1]]).then_inc(T.sem.ldf, 16)
-    g.scalar.dma_start(T.a_sb[:, span[1][0]:span[1][1]], T.a[:, span[1][0]:span[1][1]]).then_inc(T.sem.ldn, 16)
-    g.tensor.wait_ge(T.sem.ldw, 16)
-    n = 0
     for c, call in enumerate(calls):
-        g.tensor.wait_ge(T.sem.ldf if c == 0 else T.sem.ldn, 16)
-        for (H, x, sl, m) in call:
-            lo, hi = cols(H)
-            ps = T["ps%d" % n]
-            for q in range(lo, hi, B):
-                g.tensor.matmul(ps[:, q - lo:q - lo + B], T.a_sb[:, q:q + B], T.w_sb[:], True, True).then_inc(T.sem["mm%d" % n], 1)
-            g.vector.wait_ge(T.sem["mm%d" % n], (hi - lo) // B)
-            g.vector.tensor_copy(T.bund[:, lo:hi], ps[:, 0:hi - lo]).then_inc(T.sem.cpf if c == 0 else T.sem.cpn, 1)
-            n += 1
+        base = c * (G + P)
+        sem = T.sem.ldf if c == 0 else T.sem.ldn
+        qa, qb = (g.sync, g.scalar) if c == 0 else (g.scalar, g.sync)
+        lo0, hi0 = cols(call[0][0])
+        lo1, hi1 = cols(call[1][0])
+        qa.dma_start(T.ab[:, base + G:base + P], T.w[:]).then_inc(sem, 16)
+        qb.dma_start(T.ab[:, base + P:base + P + G], T.a[:, lo1:hi1]).then_inc(sem, 16)
+        qa.dma_start(T.ab[:, base:base + G], T.a[:, lo0:hi0]).then_inc(sem, 16)
     total = 0
     for c, call in enumerate(calls):
-        g.wait_ge(T.sem.cpf if c == 0 else T.sem.cpn, len(call))
+        base = c * (G + P)
+        g.wait_ge(T.sem.ldf if c == 0 else T.sem.ldn, 48)
         trs = []
-        for (H, x, sl, m) in call:
-            lo, hi = cols(H)
+        for q, (H, x, sl, m) in enumerate(call):
             trs.append(RemoteDMATransfer(dst_ids=[_dst(topo, x, core)], dma_engine_mask=m, remote_sem=T.sem["got%d" % sl],
-                                         src=T.bund[:, lo:hi], dst=T.land[:, sl * (hi - lo):(sl + 1) * (hi - lo)]))
+                                         src=T.ab[:, base + q * G:base + q * G + P], dst=T.land[:, sl * P:(sl + 1) * P]))
             total += _pop(m)
         g.remote_dma_fused(trs, local_sem=T.sem.sent)
     H = topo.host(core)

@@ -164,15 +164,15 @@ def _rank(g, core, T, topo, p):
         qa, qb = (g.sync, g.scalar) if c == 0 else (g.scalar, g.sync)
         lo0, hi0 = cols(call[0][0])
         lo1, hi1 = cols(call[1][0])
-        qa.dma_start(T.ab[:, base + G:base + P], T.w[:]).then_inc(sem, 16)
-        qb.dma_start(T.ab[:, base + P:base + P + G], T.a[:, lo1:hi1]).then_inc(sem, 16)
         qa.dma_start(T.ab[:, base:base + G], T.a[:, lo0:hi0]).then_inc(sem, 16)
+        qb.dma_start(T.ab[:, base + P:base + P + G], T.a[:, lo1:hi1]).then_inc(sem, 16)
+        qa.dma_start(T.ab[:, base + G:base + P], T.w[:]).then_inc(sem, 16)
     total = 0
     for c, call in enumerate(calls):
         base = c * (G + P)
         g.wait_ge(T.sem.ldf if c == 0 else T.sem.ldn, 48)
         trs = []
-        for q, (H, x, sl, m) in enumerate(call):
+        for q, (H, x, sl, m) in sorted(enumerate(call), key=lambda e: p["same_chip"](e[1][1], core)):
             trs.append(RemoteDMATransfer(dst_ids=[_dst(topo, x, core)], dma_engine_mask=m, remote_sem=T.sem["got%d" % sl],
                                          src=T.ab[:, base + q * G:base + q * G + P], dst=T.land[:, sl * P:(sl + 1) * P]))
             total += _pop(m)

from concourse.bass import DstId, RemoteDMATransfer
from concourse.mybir import dt, AluOpType

NSIM = 512
B = 128
G = 3 * B
P = G + B

SCRATCH = {
    "ab": ("sbuf", [128, 2 * (G + P)], "bfloat16"),
    "land": ("sbuf", [128, 2 * P], "bfloat16"),
    "bund": ("sbuf", [128, G], "bfloat16"),
    "fin": ("sbuf", [128, 6 * B], "bfloat16"),
    "y_sb": ("sbuf", [128, B], "bfloat16"),
    "ps0": ("psum", [128, 512], "float32"),
    "ps1": ("psum", [128, 512], "float32"),
    "ps2": ("psum", [128, 512], "float32"),
    "ps4": ("psum", [128, 512], "float32"),
}
SEMAPHORES = ["ldf", "ldn", "mm0", "mm1", "mm2", "sent", "vs", "st",
              "got0", "got1", "arr0", "arr1", "arr2", "arr3", "arr4", "arr5"]

_CACHE = {}


def _pop(m):
    return bin(m).count("1")


def _bits(m):
    return [1 << i for i in range(m.bit_length()) if (m >> i) & 1]


def _split(bits, n):
    L = len(bits)
    sizes = {1: [L], 2: [L // 2] * 2, 3: [L // 2, L // 4, L // 4], 4: [L // 4] * 4}[n]
    out, p = [], 0
    for s in sizes:
        out.append(sum(bits[p:p + s]))
        p += s
    return out


def _masks(topo, src, dsts):
    full = [topo.mask(src, d) for d in dsts]
    tight = min(full, key=_pop)
    res = [0] * len(dsts)
    out = [i for i, m in enumerate(full) if m == tight]
    loc = [i for i, m in enumerate(full) if m != tight]
    for i, m in zip(out, _split(_bits(tight), len(out))):
        res[i] = m
    if loc:
        for i, m in zip(loc, _split(_bits(full[loc[0]] & ~tight), len(loc))):
            res[i] = m
    return res


def _plan(T, topo):
    if "p" in _CACHE:
        return _CACHE["p"]
    cores = list(T.cores)
    hosts = sorted({topo.host(c) for c in cores})
    members = {H: [c for c in cores if topo.host(c) == H] for H in hosts}

    def rack(c):
        return topo.rack(topo.host(c))

    def same_chip(x, y):
        return topo.host(x) == topo.host(y) and topo.chip(x) == topo.chip(y)

    def hops(c, d):
        if same_chip(c, d):
            return 0
        if rack(c) == rack(d):
            return 1 if (topo.mates(c, d) or topo.same_plane(c, d)) else 2
        twin = [x for x in range(NSIM) if topo.host(x) == topo.host(d) and topo.chip(x) == topo.chip(c)][0]
        return 1 + hops(twin, d)

    pairs = []
    for R in sorted({rack(c) for c in cores}):
        left = [c for c in cores if rack(c) == R]
        while left:
            k = [c for c in left if c == left[0] or (topo.chip(c) == topo.chip(left[0]) and topo.may_write(left[0], c))]
            pairs.append(k)
            left = [c for c in left if c not in k]

    used, load, agg = set(cores), {}, {}
    for far in (True, False):
        for ci, k in enumerate(pairs):
            for H in hosts:
                if (topo.rack(H) != rack(k[0])) != far:
                    continue
                cand = [x for x in range(NSIM) if x not in used and any(same_chip(x, s) for s in k)
                        and all(topo.may_write(x, d) for d in members[H]) and all(topo.may_write(s, x) for s in k)]
                best = min(cand, key=lambda x: (load.get((topo.host(x), topo.chip(x)), 0),
                                                sum(hops(x, d) for d in members[H]),
                                                topo.die(x) != topo.die(k[0]), x))
                used.add(best)
                load[(topo.host(best), topo.chip(best))] = load.get((topo.host(best), topo.chip(best)), 0) + 1
                agg[(ci, H)] = best

    hop1 = {}
    for ci, k in enumerate(pairs):
        for slot, s in enumerate(k):
            calls = []
            for far in (True, False):
                hs = [H for H in hosts if (topo.rack(H) != rack(s)) == far]
                ms = _masks(topo, s, [agg[(ci, H)] for H in hs])
                calls.append([(H, agg[(ci, H)], slot, m) for H, m in zip(hs, ms)])
            hop1[s] = calls
    hop2 = {}
    for (ci, H), x in agg.items():
        order = sorted(range(len(members[H])), key=lambda j: (-hops(x, members[H][j]), j))
        ms = _masks(topo, x, [members[H][j] for j in order])
        hop2[x] = (ci, H, [(j, members[H][j], m) for j, m in zip(order, ms)])
    p = dict(hosts=hosts, members=members, pairs=pairs, agg=agg, hop1=hop1, hop2=hop2, same_chip=same_chip, rack=rack, hops=hops)
    _CACHE["p"] = p
    return p


def _dst(topo, d, src):
    rid, pid = topo.addr(d, src)
    return DstId(rid=rid, pnc=pid)


def _aggregator(g, core, T, topo, p):
    ci, H, sends = p["hop2"][core]
    k = p["pairs"][ci]
    n = len(k)
    cnt = [[_pop(m) for call in p["hop1"][s] for (h, x, sl, m) in call if x == core][0] for s in k]
    pos = [[q for call in p["hop1"][s] for q, (h, x, sl, m) in enumerate(call) if x == core][0] for s in k]
    order = sorted(range(n), key=lambda i: (not p["same_chip"](k[i], core), i))
    js = [j for (j, d, m) in sends]
    for t, i in enumerate(order):
        g.tensor.wait_ge(T.sem["got%d" % i], cnt[i])
        a0 = i * P + (0 if pos[i] == 0 else B)
        w0 = i * P + (G if pos[i] == 0 else 0)
        for j in js:
            mm = g.tensor.matmul(T["ps%d" % j][:, 0:B], T.land[:, a0 + j * B:a0 + (j + 1) * B], T.land[:, w0:w0 + B],
                                 t == 0, t == n - 1)
            if t == n - 1:
                mm.then_inc(T.sem["mm%d" % j], 1)
    for j in js:
        g.vector.wait_ge(T.sem["mm%d" % j], 1)
        g.vector.tensor_copy(T.bund[:, j * B:(j + 1) * B], T["ps%d" % j][:, 0:B]).then_inc(T.sem.vs, 1)
    g.wait_ge(T.sem.vs, len(js))
    g.remote_dma_fused([RemoteDMATransfer(dst_ids=[_dst(topo, d, core)], dma_engine_mask=m, remote_sem=T.sem["arr%d" % ci],
                                          src=T.bund[:, j * B:(j + 1) * B], dst=T.fin[:, ci * B:(ci + 1) * B])
                        for (j, d, m) in sends], local_sem=T.sem.sent)
    g.wait_ge(T.sem.sent, sum(_pop(m) for (j, d, m) in sends))


def _rank(g, core, T, topo, p):
    members, pairs = p["members"], p["pairs"]
    calls = p["hop1"][core]

    def cols(H):
        r0 = T.rank_of(members[H][0])
        return r0 * B, r0 * B + G

    for c, call in enumerate(calls):
        base = c * (G + P)
        sem = T.sem.ldf if c == 0 else T.sem.ldn
        qa, qb = (g.sync, g.scalar) if c == 0 else (g.scalar, g.sync)
        lo0, hi0 = cols(call[0][0])
        lo1, hi1 = cols(call[1][0])
        qa.dma_start(T.ab[:, base:base + G], T.a[:, lo0:hi0]).then_inc(sem, 16)
        qb.dma_start(T.ab[:, base + P:base + P + G], T.a[:, lo1:hi1]).then_inc(sem, 16)
        qa.dma_start(T.ab[:, base + G:base + P], T.w[:]).then_inc(sem, 16)
    total = 0
    for c, call in enumerate(calls):
        base = c * (G + P)
        g.wait_ge(T.sem.ldf if c == 0 else T.sem.ldn, 48)
        trs = []
        for q, (H, x, sl, m) in sorted(enumerate(call), key=lambda e: p["same_chip"](e[1][1], core)):
            trs.append(RemoteDMATransfer(dst_ids=[_dst(topo, x, core)], dma_engine_mask=m, remote_sem=T.sem["got%d" % sl],
                                         src=T.ab[:, base + q * G:base + q * G + P], dst=T.land[:, sl * P:(sl + 1) * P]))
            total += _pop(m)
        g.remote_dma_fused(trs, local_sem=T.sem.sent)
    H = topo.host(core)
    cnt = {}
    for ci in range(len(pairs)):
        cnt[ci] = [_pop(m) for (j, d, m) in p["hop2"][p["agg"][(ci, H)]][2] if d == core][0]
    order = sorted(range(len(pairs)), key=lambda ci: (p["rack"](pairs[ci][0]) != p["rack"](core),
                                                      p["hops"](p["agg"][(ci, H)], core), -cnt[ci], ci))
    v = g.vector
    f = [T.fin[:, ci * B:(ci + 1) * B] for ci in order]
    v.wait_ge(T.sem["arr%d" % order[0]], cnt[order[0]])
    v.wait_ge(T.sem["arr%d" % order[1]], cnt[order[1]])
    v.tensor_tensor(T.ps4[:, 0:B], f[0], f[1], AluOpType.add).then_inc(T.sem.vs, 1)
    for t in range(2, len(order)):
        v.wait_ge(T.sem["arr%d" % order[t]], cnt[order[t]])
        v.wait_ge(T.sem.vs, t - 1)
        out = T.y_sb[:] if t == len(order) - 1 else T.ps4[:, (t - 1) * B:t * B]
        v.tensor_tensor(out, T.ps4[:, (t - 2) * B:(t - 1) * B], f[t], AluOpType.add).then_inc(T.sem.vs, 1)
    g.sync.wait_ge(T.sem.vs, len(order) - 1)
    g.sync.dma_start(T.y[:], T.y_sb[:]).then_inc(T.sem.st, 16)
    g.sync.wait_ge(T.sem.st, 16)
    g.wait_ge(T.sem.sent, total)


def rank_program(g, core, T, topo):
    p = _plan(T, topo)
    if T.rank_of(core) is not None:
        _rank(g, core, T, topo, p)
    elif core in p["hop2"]:
        _aggregator(g, core, T, topo, p)
